import numpy as np
import ml_dtypes


def mxq(x, axis, fmt="e4m3"):
    dtype, down = {"e4m3": (ml_dtypes.float8_e4m3fn, 7), "e5m2": (ml_dtypes.float8_e5m2, 14)}[fmt]
    v = np.moveaxis(np.asarray(x, np.float32).astype(ml_dtypes.bfloat16).astype(np.float64), axis, -1)
    blocks = v.reshape(v.shape[:-1] + (-1, 32))
    amax = np.abs(blocks).max(-1, keepdims=True)
    byte = np.maximum(np.where(amax > 0, np.frexp(amax)[1] - 1 + 127, 0) - down, 1)
    scale = np.exp2(byte - 127.0)
    codes = (blocks / scale).astype(np.float32).astype(dtype).astype(np.float64)
    return np.moveaxis((codes * scale).reshape(v.shape), -1, axis)


WIDE = False


def mx_kscale(k):
    if not WIDE:
        return np.ones(k)
    levels = np.array([10, -10, 5, -5, 0])
    if k % 512:
        return np.exp2(np.random.permutation(np.resize(levels, k // 32))).repeat(32)
    a = np.empty((k // 512, 16))
    for p in range(k // 512):
        a[p, :8] = np.random.permutation(np.resize(levels, 8))
        for g in range(8):
            far = levels[np.abs(levels - a[p, g]) >= 10]
            a[p, g + 8] = far[np.random.randint(len(far))]
    return np.exp2(a.ravel()).repeat(32)


def f64(x):
    return np.asarray(x).astype(np.float64)


def striped(idx):
    return np.tile(idx.reshape(-1, 16).T, (8, 1)).astype(np.uint16)


def unstriped(offs):
    return offs[:16].T.reshape(-1).astype(np.int64)


def pack_weight(w):
    k, n = w.shape
    w = f64(np.asarray(w, np.float32).astype(ml_dtypes.bfloat16)).reshape(k // 32, 32, n)
    amax = np.abs(w).max(1)
    byte = np.clip(np.where(amax > 0, np.frexp(amax)[1] - 1 + 127 - 7, 1), 1, 254)
    scaled = (w * np.exp2(127.0 - byte)[:, None, :]).reshape(k, n).astype(np.float32)
    words = np.ascontiguousarray(scaled.reshape(k // 512, 128, 4, n).transpose(0, 1, 3, 2)).astype(ml_dtypes.float8_e4m3fn).view(np.uint8)
    return words, np.ascontiguousarray(byte.astype(np.uint8).reshape(k // 512, 16, n))


def unpack_weight(words, scales):
    g, p, n, _ = words.shape
    vals = np.ascontiguousarray(words).view(ml_dtypes.float8_e4m3fn).astype(np.float64) * np.repeat(np.exp2(scales.astype(np.float64) - 127.0), 8, axis=1)[..., None]
    return vals.transpose(0, 1, 3, 2).reshape(g * 512, n)


def relu(v):
    return np.maximum(v, 0.0)


K, T, S, D, V, N = 1024, 2048, 1024, 3, 512, 256
P = 2 ** 7


def setup_inputs():
    n = np.random.standard_normal
    s = mx_kscale(K)[:, None]
    packed_xT = pack_weight(n((K, T)) * s)
    return {
        "x_words": packed_xT[0],
        "x_scales": packed_xT[1],
        "w1": (n((K, N)) / np.sqrt(K) / s).astype(np.float32),
        "score": np.tile(np.random.standard_normal((D, 1, V)), (1, P, 1)).astype(np.float32),
        "offs": striped(np.random.permutation(T)[:S]),
        "pos1": striped(np.random.permutation(S)[:V]),
        "pos2": striped(np.random.permutation(S)[:V]),
        "pos3": striped(np.random.permutation(S)[:V]),
    }


def reference(x_words, x_scales, w1, score, offs, pos1, pos2, pos3):
    xq = unpack_weight(x_words, x_scales)[:, unstriped(offs)]
    y = mxq(f64(w1), 0, "e4m3").T @ xq
    e0 = np.exp(f64(score)[0, :1])
    e1 = np.exp(f64(score)[1, :1])
    e2 = np.exp(f64(score)[2, :1])
    num = y[:, unstriped(pos1)] * e0 + y[:, unstriped(pos2)] * e1 + y[:, unstriped(pos3)] * e2
    den = e0 + e1 + e2
    return relu(num / den)

@@ -1,0 +1,186 @@
+from contextlib import ExitStack
+
+import concourse.mybir as mybir
+from concourse.masks import make_identity
+
+K, T, S, D, V, N = 1024, 2048, 1024, 3, 512, 256
+P = 128
+PACK = 4
+PASSES = K // (P * PACK)
+BLOCKS = N // P
+LANES = 16
+FLOPS = 2 * K * S * N
+BYTES = K * T + K // 32 * T + 4 * K * N + 4 * D * V + 2 * P * (S + D * V) // LANES + 4 * N * V
+
+F32 = mybir.dt.float32
+BF16 = mybir.dt.bfloat16
+I32 = mybir.dt.int32
+U32 = mybir.dt.uint32
+U16 = mybir.dt.uint16
+U8 = mybir.dt.uint8
+FP8X4 = mybir.dt.float8_e4m3fn_x4
+ALU = mybir.AluOpType
+ACT = mybir.ActivationFunctionType
+AX = mybir.AxisListType
+
+LAST_PASS_PIECES = ((0, 512), (512, 768), (768, 1024))
+
+
+def entries(list_tile, lo, hi):
+    return list_tile[:, lo // LANES : hi // LANES]
+
+
+def tile_picked_gatv_relu_p_kernel(tc, x_words, x_scales, w1, score, offs, pos1, pos2, pos3, out):
+    nc = tc.nc
+    with ExitStack() as ctx:
+        sb = ctx.enter_context(tc.tile_pool(name="sb", bufs=1))
+        ps = ctx.enter_context(tc.psum_pool(name="ps", bufs=1))
+
+        scale_table = sb.tile([P, T], U8, name="scale_table", align_bytes=64)
+        nc.vector.memset(scale_table[:].bitcast(I32), 0)
+        for q in range(4):
+            nc.scalar.dma_start(
+                out=scale_table[32 * q : 32 * q + 4 * PASSES, :].bitcast(I32),
+                in_=x_scales[:, 4 * q : 4 * q + 4, :].bitcast(I32),
+            )
+        warm_in = sb.tile([P, 1], F32, name="warm_in")
+        nc.vector.memset(warm_in[:], 0.0)
+        warm_out = sb.tile([P, 1], F32, name="warm_out")
+        nc.scalar.activation(warm_out[:], warm_in[:], ACT.Exp)
+
+        scores = sb.tile([P, D, PACK], F32, name="scores")
+        nc.sync.dma_start(out=scores[:], in_=score[:, 0, :].rearrange("d (p j) -> p d j", j=PACK))
+        picked = sb.tile([P, S // LANES], U16, name="picked")
+        nc.sync.dma_start(picked[:], offs)
+
+        word_table = [sb.tile([P, T], I32, name=f"word_table{z}", align_bytes=64) for z in range(PASSES)]
+        w_raw = [sb.tile([P, PACK, N], F32, name=f"w_raw{z}") for z in range(PASSES)]
+
+        def load_words(z):
+            nc.sync.dma_start(out=word_table[z][:], in_=x_words[z].rearrange("p n t -> p (n t)").bitcast(I32))
+
+        load_words(0)
+        for z in range(PASSES):
+            rows = w1[z * P * PACK : (z + 1) * P * PACK, :]
+            nc.sync.dma_start(out=w_raw[z][:], in_=rows.rearrange("(p j) m -> p j m", j=PACK))
+        load_words(1)
+        neighbours = []
+        for d, pos in enumerate((pos1, pos2, pos3)):
+            places = sb.tile([P, V // LANES], U16, name=f"places{d}")
+            nc.sync.dma_start(places[:], pos)
+            neighbours.append(places)
+
+        ident = sb.tile([P, P], F32, name="ident")
+        make_identity(nc, ident[:])
+
+        top = sb.tile([P, PACK], F32, name="top")
+        nc.vector.tensor_reduce(top[:], scores[:].rearrange("p d j -> p j d"), AX.X, ALU.max)
+        shifted = sb.tile([P, D, PACK], F32, name="shifted")
+        nc.vector.tensor_tensor(shifted[:], scores[:], top[:].unsqueeze(1).to_broadcast([P, D, PACK]), ALU.subtract)
+        expd = sb.tile([P, D, PACK], F32, name="expd")
+        nc.scalar.activation(expd[:], shifted[:], ACT.Exp)
+        total = sb.tile([P, PACK], F32, name="total")
+        nc.vector.tensor_reduce(total[:], expd[:].rearrange("p d j -> p j d"), AX.X, ALU.add)
+        inverse = sb.tile([P, PACK], F32, name="inverse", tag="inverse_then_x_scale", align_bytes=64)
+        nc.vector.reciprocal(inverse[:], total[:])
+        alpha = sb.tile([P, D, PACK], F32, name="alpha")
+        nc.vector.tensor_tensor(alpha[:], expd[:], inverse[:].unsqueeze(1).to_broadcast([P, D, PACK]), ALU.mult)
+
+        x_scale = sb.tile([P, S], U8, name="x_scale", tag="inverse_then_x_scale", align_bytes=64)
+        nc.vector.tensor_copy(x_scale[:], scale_table[:].indirect(picked[:]))
+        x_codes = [sb.tile([P, S], U32, name=f"x_codes{z}", align_bytes=64) for z in range(PASSES)]
+        nc.vector.tensor_copy(x_codes[0][:], word_table[0][:].bitcast(U32).indirect(picked[:]))
+
+        w_codes, w_scale = [], []
+
+        def round_weights(b):
+            grouped = sb.tile([P, PASSES, P, PACK], BF16, name=f"grouped{b}", align_bytes=64)
+            for z in range(PASSES):
+                nc.scalar.copy(
+                    grouped[:, z].rearrange("p (c i) j -> p c j i", i=4),
+                    w_raw[z][:, :, b * P : (b + 1) * P].rearrange("p j (c i) -> p c j i", i=4),
+                )
+            return grouped
+
+        def quantise_weights(b, grouped):
+            codes = sb.tile([P, PASSES * P], U32, name=f"w_codes{b}", align_bytes=64)
+            plane = sb.tile([P, PASSES * P], U8, name=f"w_scale{b}", align_bytes=64)
+            nc.vector.quantize_mx(out=codes[:].bitcast(FP8X4), scales=plane[:], in_=grouped[:].rearrange("p z m j -> p (z m j)"))
+            w_codes.append(codes)
+            w_scale.append(plane)
+
+        def product_pass(acc, b, z, lo, hi):
+            nc.tensor.matmul_mx(
+                out=acc,
+                lhsT=w_codes[b][:, z * P : (z + 1) * P].bitcast(FP8X4),
+                lhsT_scale=w_scale[b][:, z * P : (z + 1) * P],
+                rhs=x_codes[z][:, lo:hi].bitcast(FP8X4),
+                rhs_scale=x_scale[4 * z : P, lo:hi],
+                start=(z == 0),
+                stop=(z == PASSES - 1),
+            )
+
+        grouped0 = round_weights(0)
+        quantise_weights(0, grouped0)
+        grouped1 = round_weights(1)
+
+        alpha_rows = []
+        for d in range(D):
+            spread = ps.tile([P, PACK, P], F32, name=f"spread{d}", tag=f"aux{d}")
+            for j in range(PACK):
+                nc.tensor.transpose(spread[:, j, :], alpha[:, d, j : j + 1].to_broadcast([P, P]), ident[:])
+            row = sb.tile([P, V], F32, name=f"alpha_row{d}")
+            nc.scalar.copy(row[:].rearrange("p (n j) -> p n j", j=PACK), spread[:].rearrange("p j n -> p n j"))
+            alpha_rows.append(row)
+
+        y = [sb.tile([P, S], F32, name=f"y{b}") for b in range(BLOCKS)]
+        acc0 = [ps.tile([P, hi - lo], F32, name=f"acc0_{lo}") for lo, hi in LAST_PASS_PIECES]
+        for acc, (lo, hi) in zip(acc0, LAST_PASS_PIECES):
+            product_pass(acc[:], 0, 0, lo, hi)
+        for acc, (lo, hi) in zip(acc0, LAST_PASS_PIECES):
+            nc.vector.tensor_copy(x_codes[1][:, lo:hi], word_table[1][:].bitcast(U32).indirect(entries(picked, lo, hi)))
+            product_pass(acc[:], 0, 1, lo, hi)
+            nc.scalar.copy(y[0][:, lo:hi], acc[:])
+        quantise_weights(1, grouped1)
+        for lo in range(0, S, 512):
+            acc = ps.tile([P, 512], F32, name=f"acc1_{lo}")
+            for z in range(PASSES):
+                product_pass(acc[:], 1, z, lo, lo + 512)
+            nc.scalar.copy(y[1][:, lo : lo + 512], acc[:])
+
+        def weighted(term, b, d, lo, hi):
+            nc.vector.tensor_tensor(term[:, lo:hi], y[b][:].indirect(entries(neighbours[d], lo, hi)), alpha_rows[d][:, lo:hi], ALU.mult)
+
+        chunks = V // P
+        turned = ps.tile([P, chunks, P], F32, name="turned", tag="aux0")
+        for d in range(D):
+            term = sb.tile([P, V], F32, name=f"term0_{d}")
+            weighted(term, 0, d, 0, V)
+            for c in range(chunks):
+                nc.tensor.matmul(
+                    turned[:, c, :], term[:, c * P : (c + 1) * P], ident[:], is_transpose=True,
+                    start=(d == 0 and c == 0), stop=(d == D - 1 and c == chunks - 1),
+                )
+        rectified = sb.tile([P, V], F32, name="rectified")
+        nc.scalar.activation(rectified[:], turned[:].rearrange("p c m -> p (c m)"), ACT.Relu)
+        back = ps.tile([P, chunks, P], F32, name="back", tag="aux1")
+        for c in range(chunks):
+            nc.tensor.transpose(back[:, c, :], rectified[:, c * P : (c + 1) * P], ident[:])
+        result0 = sb.tile([P, V], F32, name="result0")
+        nc.scalar.copy(result0[:], back[:].rearrange("p c v -> p (c v)"))
+        nc.sync.dma_start(out=out[0:P, :], in_=result0[:])
+
+        terms = [sb.tile([P, V], F32, name=f"term1_{d}") for d in range(D)]
+        half = V // 2
+        weighted(terms[0], 1, 0, 0, V)
+        weighted(terms[1], 1, 1, 0, V)
+        weighted(terms[2], 1, 2, 0, half)
+        partial = sb.tile([P, V], F32, name="partial")
+        nc.vector.tensor_tensor(partial[:], terms[0][:], terms[1][:], ALU.add)
+        weighted(terms[2], 1, 2, half, V)
+        for lo in (0, half):
+            summed = sb.tile([P, half], F32, name=f"summed{lo}")
+            nc.vector.tensor_tensor(summed[:], partial[:, lo : lo + half], terms[2][:, lo : lo + half], ALU.add)
+            result1 = sb.tile([P, half], F32, name=f"result1_{lo}")
+            nc.scalar.activation(result1[:], summed[:], ACT.Relu)
+            nc.sync.dma_start(out=out[P : 2 * P, lo : lo + half], in_=result1[:])

@@ -23,7 +23,7 @@ ALU = mybir.AluOpType
 ACT = mybir.ActivationFunctionType
 AX = mybir.AxisListType
 
-LAST_PASS_PIECES = ((0, 512), (512, 768), (768, 1024))
+PIECES = ((0, 512), (512, 768), (768, 1024))
 
 
 def entries(list_tile, lo, hi):
@@ -37,92 +37,60 @@ def tile_picked_gatv_relu_p_kernel(tc, x_words, x_scales, w1, score, offs, pos1,
         ps = ctx.enter_context(tc.psum_pool(name="ps", bufs=1))
 
         scale_table = sb.tile([P, T], U8, name="scale_table", align_bytes=64)
-        nc.vector.memset(scale_table[:].bitcast(I32), 0)
-        for q in range(4):
-            nc.scalar.dma_start(
-                out=scale_table[32 * q : 32 * q + 4 * PASSES, :].bitcast(I32),
-                in_=x_scales[:, 4 * q : 4 * q + 4, :].bitcast(I32),
-            )
+        nc.gpsimd.memset(scale_table[:].bitcast(I32), 0)
+
+        def load_scales():
+            for q in range(4):
+                nc.sync.dma_start(
+                    out=scale_table[32 * q : 32 * q + 4 * PASSES, :].bitcast(I32),
+                    in_=x_scales[:, 4 * q : 4 * q + 4, :].bitcast(I32),
+                )
+
+        def load_list(name, source):
+            list_tile = sb.tile(list(source.shape), U16, name=name)
+            nc.sync.dma_start(list_tile[:], source)
+            return list_tile
+
+        word_table = [sb.tile([P, T], I32, name=f"word_table{z}", align_bytes=64) for z in range(PASSES)]
+        w_raw = [sb.tile([P, PACK, N], F32, name=f"w_raw{z}") for z in range(PASSES)]
+
+        def load_pass(z):
+            nc.sync.dma_start(out=word_table[z][:], in_=x_words[z].rearrange("p n t -> p (n t)").bitcast(I32))
+            rows = w1[z * P * PACK : (z + 1) * P * PACK, :]
+            nc.sync.dma_start(out=w_raw[z][:], in_=rows.rearrange("(p j) m -> p j m", j=PACK))
+
+        scores = sb.tile([P, D, 2 * PACK], F32, name="scores")[:, :, 0:PACK]
+        nc.sync.dma_start(out=scores, in_=score[:, 0, :].rearrange("d (p j) -> p d j", j=PACK))
+        picked = load_list("picked", offs)
+        neighbours = [load_list("places0", pos1)]
+        load_scales()
+        load_pass(0)
+        load_pass(1)
+        neighbours.append(load_list("places1", pos2))
+        neighbours.append(load_list("places2", pos3))
+
         warm_in = sb.tile([P, 1], F32, name="warm_in")
         nc.vector.memset(warm_in[:], 0.0)
         warm_out = sb.tile([P, 1], F32, name="warm_out")
         nc.scalar.activation(warm_out[:], warm_in[:], ACT.Exp)
 
-        scores = sb.tile([P, D, PACK], F32, name="scores")
-        nc.sync.dma_start(out=scores[:], in_=score[:, 0, :].rearrange("d (p j) -> p d j", j=PACK))
-        picked = sb.tile([P, S // LANES], U16, name="picked")
-        nc.sync.dma_start(picked[:], offs)
-
-        word_table = [sb.tile([P, T], I32, name=f"word_table{z}", align_bytes=64) for z in range(PASSES)]
-        w_raw = [sb.tile([P, PACK, N], F32, name=f"w_raw{z}") for z in range(PASSES)]
-
-        def load_words(z):
-            nc.sync.dma_start(out=word_table[z][:], in_=x_words[z].rearrange("p n t -> p (n t)").bitcast(I32))
-
-        load_words(0)
-        for z in range(PASSES):
-            rows = w1[z * P * PACK : (z + 1) * P * PACK, :]
-            nc.sync.dma_start(out=w_raw[z][:], in_=rows.rearrange("(p j) m -> p j m", j=PACK))
-        load_words(1)
-        neighbours = []
-        for d, pos in enumerate((pos1, pos2, pos3)):
-            places = sb.tile([P, V // LANES], U16, name=f"places{d}")
-            nc.sync.dma_start(places[:], pos)
-            neighbours.append(places)
-
         ident = sb.tile([P, P], F32, name="ident")
         make_identity(nc, ident[:])
 
-        top = sb.tile([P, PACK], F32, name="top")
-        nc.vector.tensor_reduce(top[:], scores[:].rearrange("p d j -> p j d"), AX.X, ALU.max)
-        shifted = sb.tile([P, D, PACK], F32, name="shifted")
-        nc.vector.tensor_tensor(shifted[:], scores[:], top[:].unsqueeze(1).to_broadcast([P, D, PACK]), ALU.subtract)
-        expd = sb.tile([P, D, PACK], F32, name="expd")
-        nc.scalar.activation(expd[:], shifted[:], ACT.Exp)
-        total = sb.tile([P, PACK], F32, name="total")
-        nc.vector.tensor_reduce(total[:], expd[:].rearrange("p d j -> p j d"), AX.X, ALU.add)
-        inverse = sb.tile([P, PACK], F32, name="inverse", tag="inverse_then_x_scale", align_bytes=64)
-        nc.vector.reciprocal(inverse[:], total[:])
+        shape = [P, D, PACK, D]
+        gaps = sb.tile(shape, F32, name="gaps")
+        nc.vector.tensor_tensor(
+            gaps[:],
+            scores.rearrange("p r j -> p j r").unsqueeze(1).to_broadcast(shape),
+            scores.unsqueeze(3).to_broadcast(shape),
+            ALU.subtract,
+        )
+        ratios = sb.tile(shape, F32, name="ratios", tag="ratios_then_x_scale", align_bytes=64)
+        nc.scalar.activation(ratios[:], gaps[:], ACT.Exp)
+        total = sb.tile([P, D, PACK], F32, name="total")
+        nc.vector.tensor_reduce(total[:], ratios[:], AX.X, ALU.add)
         alpha = sb.tile([P, D, PACK], F32, name="alpha")
-        nc.vector.tensor_tensor(alpha[:], expd[:], inverse[:].unsqueeze(1).to_broadcast([P, D, PACK]), ALU.mult)
-
-        x_scale = sb.tile([P, S], U8, name="x_scale", tag="inverse_then_x_scale", align_bytes=64)
-        nc.vector.tensor_copy(x_scale[:], scale_table[:].indirect(picked[:]))
-        x_codes = [sb.tile([P, S], U32, name=f"x_codes{z}", align_bytes=64) for z in range(PASSES)]
-        nc.vector.tensor_copy(x_codes[0][:], word_table[0][:].bitcast(U32).indirect(picked[:]))
-
-        w_codes, w_scale = [], []
-
-        def round_weights(b):
-            grouped = sb.tile([P, PASSES, P, PACK], BF16, name=f"grouped{b}", align_bytes=64)
-            for z in range(PASSES):
-                nc.scalar.copy(
-                    grouped[:, z].rearrange("p (c i) j -> p c j i", i=4),
-                    w_raw[z][:, :, b * P : (b + 1) * P].rearrange("p j (c i) -> p c j i", i=4),
-                )
-            return grouped
-
-        def quantise_weights(b, grouped):
-            codes = sb.tile([P, PASSES * P], U32, name=f"w_codes{b}", align_bytes=64)
-            plane = sb.tile([P, PASSES * P], U8, name=f"w_scale{b}", align_bytes=64)
-            nc.vector.quantize_mx(out=codes[:].bitcast(FP8X4), scales=plane[:], in_=grouped[:].rearrange("p z m j -> p (z m j)"))
-            w_codes.append(codes)
-            w_scale.append(plane)
-
-        def product_pass(acc, b, z, lo, hi):
-            nc.tensor.matmul_mx(
-                out=acc,
-                lhsT=w_codes[b][:, z * P : (z + 1) * P].bitcast(FP8X4),
-                lhsT_scale=w_scale[b][:, z * P : (z + 1) * P],
-                rhs=x_codes[z][:, lo:hi].bitcast(FP8X4),
-                rhs_scale=x_scale[4 * z : P, lo:hi],
-                start=(z == 0),
-                stop=(z == PASSES - 1),
-            )
-
-        grouped0 = round_weights(0)
-        quantise_weights(0, grouped0)
-        grouped1 = round_weights(1)
+        nc.vector.reciprocal(alpha[:], total[:])
 
         alpha_rows = []
         for d in range(D):
@@ -133,54 +101,107 @@ def tile_picked_gatv_relu_p_kernel(tc, x_words, x_scales, w1, score, offs, pos1,
             nc.scalar.copy(row[:].rearrange("p (n j) -> p n j", j=PACK), spread[:].rearrange("p j n -> p n j"))
             alpha_rows.append(row)
 
+        x_scale = sb.tile([P, S], U8, name="x_scale", tag="ratios_then_x_scale", align_bytes=64)
+        nc.vector.tensor_copy(x_scale[:], scale_table[:].indirect(picked[:]))
+        x_codes0 = sb.tile([P, S], U32, name="x_codes0", align_bytes=64)
+        nc.vector.tensor_copy(x_codes0[:], word_table[0][:].bitcast(U32).indirect(picked[:]))
+
+        w_codes = [sb.tile([P, PASSES * P], U32, name=f"w_codes{b}", align_bytes=64) for b in range(BLOCKS)]
+        w_scale = [sb.tile([P, PASSES * P], U8, name=f"w_scale{b}", align_bytes=64) for b in range(BLOCKS)]
+
+        def round_weights(grouped, b, z):
+            nc.scalar.copy(
+                grouped.rearrange("p (c i) j -> p c j i", i=4),
+                w_raw[z][:, :, b * P : (b + 1) * P].rearrange("p j (c i) -> p c j i", i=4),
+            )
+
+        def product_pass(acc, b, z, codes, lo, hi):
+            nc.tensor.matmul_mx(
+                out=acc,
+                lhsT=w_codes[b][:, z * P : (z + 1) * P].bitcast(FP8X4),
+                lhsT_scale=w_scale[b][:, z * P : (z + 1) * P],
+                rhs=codes.bitcast(FP8X4),
+                rhs_scale=x_scale[4 * z : P, lo:hi],
+                start=(z == 0),
+                stop=(z == PASSES - 1),
+            )
+
+        grouped1 = sb.tile([P, PASSES, P, PACK], BF16, name="grouped1", align_bytes=64)
+        for z in range(PASSES):
+            grouped0 = sb.tile([P, P, PACK], BF16, name=f"grouped0_{z}", tag=f"staged{z}", align_bytes=64)
+            round_weights(grouped0[:], 0, z)
+            cols = slice(z * P, (z + 1) * P)
+            nc.vector.quantize_mx(
+                out=w_codes[0][:, cols].bitcast(FP8X4), scales=w_scale[0][:, cols], in_=grouped0[:].rearrange("p m j -> p (m j)")
+            )
+            round_weights(grouped1[:, z], 1, z)
+
         y = [sb.tile([P, S], F32, name=f"y{b}") for b in range(BLOCKS)]
-        acc0 = [ps.tile([P, hi - lo], F32, name=f"acc0_{lo}") for lo, hi in LAST_PASS_PIECES]
-        for acc, (lo, hi) in zip(acc0, LAST_PASS_PIECES):
-            product_pass(acc[:], 0, 0, lo, hi)
-        for acc, (lo, hi) in zip(acc0, LAST_PASS_PIECES):
-            nc.vector.tensor_copy(x_codes[1][:, lo:hi], word_table[1][:].bitcast(U32).indirect(entries(picked, lo, hi)))
-            product_pass(acc[:], 0, 1, lo, hi)
-            nc.scalar.copy(y[0][:, lo:hi], acc[:])
-        quantise_weights(1, grouped1)
-        for lo in range(0, S, 512):
-            acc = ps.tile([P, 512], F32, name=f"acc1_{lo}")
-            for z in range(PASSES):
-                product_pass(acc[:], 1, z, lo, lo + 512)
-            nc.scalar.copy(y[1][:, lo : lo + 512], acc[:])
+        acc0 = [ps.tile([P, hi - lo], F32, name=f"acc0_{lo}", tag=f"acc0_{lo}") for lo, hi in PIECES]
+        for acc, (lo, hi) in zip(acc0, PIECES):
+            product_pass(acc[:], 0, 0, x_codes0[:, lo:hi], lo, hi)
+        x_codes1 = []
+        for tag, (lo, hi) in zip(("staged0", "middle", "staged1"), PIECES):
+            piece = sb.tile([P, hi - lo], U32, name=f"x_codes1_{lo}", tag=tag, align_bytes=64)
+            nc.vector.tensor_copy(piece[:], word_table[1][:].bitcast(U32).indirect(entries(picked, lo, hi)))
+            x_codes1.append(piece)
+        nc.vector.quantize_mx(
+            out=w_codes[1][:].bitcast(FP8X4), scales=w_scale[1][:], in_=grouped1[:].rearrange("p z m j -> p (z m j)")
+        )
+        for acc, piece, (lo, hi) in zip(acc0, x_codes1, PIECES):
+            product_pass(acc[:], 0, 1, piece[:], lo, hi)
+            if lo == 0:
+                nc.vector.tensor_copy(y[0][:, lo:hi], acc[:])
+            else:
+                nc.scalar.copy(y[0][:, lo:hi], acc[:])
+        for bank in range(2):
+            acc = ps.tile([P, 512], F32, name=f"acc1_{bank}")
+            for piece, (lo, hi) in zip(x_codes1, PIECES):
+                if lo // 512 == bank:
+                    part = acc[:, lo % 512 : lo % 512 + hi - lo]
+                    product_pass(part, 1, 0, x_codes0[:, lo:hi], lo, hi)
+                    product_pass(part, 1, 1, piece[:], lo, hi)
+            nc.scalar.copy(y[1][:, bank * 512 : (bank + 1) * 512], acc[:])
 
         def weighted(term, b, d, lo, hi):
-            nc.vector.tensor_tensor(term[:, lo:hi], y[b][:].indirect(entries(neighbours[d], lo, hi)), alpha_rows[d][:, lo:hi], ALU.mult)
+            nc.vector.tensor_tensor(term, y[b][:].indirect(entries(neighbours[d], lo, hi)), alpha_rows[d][:, lo:hi], ALU.mult)
 
-        chunks = V // P
-        turned = ps.tile([P, chunks, P], F32, name="turned", tag="aux0")
-        for d in range(D):
-            term = sb.tile([P, V], F32, name=f"term0_{d}")
-            weighted(term, 0, d, 0, V)
+        def sum_on_tensor(b, lo, hi, tags):
+            width = hi - lo
+            chunks = width // P
+            turned = ps.tile([P, chunks, P], F32, name=f"turned{b}", tag=tags[0])
+            for d in range(D):
+                term = sb.tile([P, width], F32, name=f"term{b}_{d}")
+                weighted(term[:], b, d, lo, hi)
+                for c in range(chunks):
+                    nc.tensor.matmul(
+                        turned[:, c, :], term[:, c * P : (c + 1) * P], ident[:], is_transpose=True,
+                        start=(d == 0 and c == 0), stop=(d == D - 1 and c == chunks - 1),
+                    )
+            rectified = sb.tile([P, width], F32, name=f"rectified{b}")
+            nc.scalar.activation(rectified[:], turned[:].rearrange("p c m -> p (c m)"), ACT.Relu)
+            back = ps.tile([P, chunks, P], F32, name=f"back{b}", tag=tags[1])
             for c in range(chunks):
-                nc.tensor.matmul(
-                    turned[:, c, :], term[:, c * P : (c + 1) * P], ident[:], is_transpose=True,
-                    start=(d == 0 and c == 0), stop=(d == D - 1 and c == chunks - 1),
-                )
-        rectified = sb.tile([P, V], F32, name="rectified")
-        nc.scalar.activation(rectified[:], turned[:].rearrange("p c m -> p (c m)"), ACT.Relu)
-        back = ps.tile([P, chunks, P], F32, name="back", tag="aux1")
-        for c in range(chunks):
-            nc.tensor.transpose(back[:, c, :], rectified[:, c * P : (c + 1) * P], ident[:])
-        result0 = sb.tile([P, V], F32, name="result0")
-        nc.scalar.copy(result0[:], back[:].rearrange("p c v -> p (c v)"))
-        nc.sync.dma_start(out=out[0:P, :], in_=result0[:])
+                nc.tensor.transpose(back[:, c, :], rectified[:, c * P : (c + 1) * P], ident[:])
+            result = sb.tile([P, width], F32, name=f"result{b}")
+            nc.scalar.copy(result[:], back[:].rearrange("p c v -> p (c v)"))
+            nc.sync.dma_start(out=out[b * P : (b + 1) * P, lo:hi], in_=result[:])
 
-        terms = [sb.tile([P, V], F32, name=f"term1_{d}") for d in range(D)]
         half = V // 2
-        weighted(terms[0], 1, 0, 0, V)
-        weighted(terms[1], 1, 1, 0, V)
-        weighted(terms[2], 1, 2, 0, half)
-        partial = sb.tile([P, V], F32, name="partial")
+        sum_on_tensor(0, 0, V, ("aux0", "aux1"))
+        sum_on_tensor(1, 0, half, ("aux2", "acc0_0"))
+
+        terms = [sb.tile([P, half], F32, name=f"last_term{d}") for d in range(D)]
+        weighted(terms[0][:], 1, 0, half, V)
+        weighted(terms[1][:], 1, 1, half, V)
+        weighted(terms[2][:, 0:P], 1, 2, half, half + P)
+        partial = sb.tile([P, half], F32, name="partial")
         nc.vector.tensor_tensor(partial[:], terms[0][:], terms[1][:], ALU.add)
-        weighted(terms[2], 1, 2, half, V)
-        for lo in (0, half):
-            summed = sb.tile([P, half], F32, name=f"summed{lo}")
-            nc.vector.tensor_tensor(summed[:], partial[:, lo : lo + half], terms[2][:, lo : lo + half], ALU.add)
-            result1 = sb.tile([P, half], F32, name=f"result1_{lo}")
-            nc.scalar.activation(result1[:], summed[:], ACT.Relu)
-            nc.sync.dma_start(out=out[P : 2 * P, lo : lo + half], in_=result1[:])
+        weighted(terms[2][:, P:half], 1, 2, half + P, V)
+        summed = sb.tile([P, half], F32, name="summed")
+        last = sb.tile([P, half], F32, name="last")
+        for lo in (0, P):
+            nc.vector.tensor_tensor(summed[:, lo : lo + P], partial[:, lo : lo + P], terms[2][:, lo : lo + P], ALU.add)
+        for lo in (0, P):
+            nc.vector.tensor_scalar_max(last[:, lo : lo + P], summed[:, lo : lo + P], 0.0)
+        nc.sync.dma_start(out=out[P : 2 * P, half:V], in_=last[:])

from contextlib import ExitStack

import concourse.mybir as mybir
from concourse.masks import make_identity

K, T, S, D, V, N = 1024, 2048, 1024, 3, 512, 256
P = 128
PACK = 4
PASSES = K // (P * PACK)
BLOCKS = N // P
LANES = 16
FLOPS = 2 * K * S * N
BYTES = K * T + K // 32 * T + 4 * K * N + 4 * D * V + 2 * P * (S + D * V) // LANES + 4 * N * V

F32 = mybir.dt.float32
BF16 = mybir.dt.bfloat16
I32 = mybir.dt.int32
U32 = mybir.dt.uint32
U16 = mybir.dt.uint16
U8 = mybir.dt.uint8
FP8X4 = mybir.dt.float8_e4m3fn_x4
ALU = mybir.AluOpType
ACT = mybir.ActivationFunctionType
AX = mybir.AxisListType

PIECES = ((0, 512), (512, 768), (768, 1024))


def entries(list_tile, lo, hi):
    return list_tile[:, lo // LANES : hi // LANES]


def tile_picked_gatv_relu_p_kernel(tc, x_words, x_scales, w1, score, offs, pos1, pos2, pos3, out):
    nc = tc.nc
    with ExitStack() as ctx:
        sb = ctx.enter_context(tc.tile_pool(name="sb", bufs=1))
        ps = ctx.enter_context(tc.psum_pool(name="ps", bufs=1))

        scale_table = sb.tile([P, T], U8, name="scale_table", align_bytes=64)
        nc.gpsimd.memset(scale_table[:].bitcast(I32), 0)

        def load_scales():
            for q in range(4):
                nc.sync.dma_start(
                    out=scale_table[32 * q : 32 * q + 4 * PASSES, :].bitcast(I32),
                    in_=x_scales[:, 4 * q : 4 * q + 4, :].bitcast(I32),
                )

        def load_list(name, source):
            list_tile = sb.tile(list(source.shape), U16, name=name)
            nc.sync.dma_start(list_tile[:], source)
            return list_tile

        word_table = [sb.tile([P, T], I32, name=f"word_table{z}", align_bytes=64) for z in range(PASSES)]
        w_raw = [sb.tile([P, PACK, N], F32, name=f"w_raw{z}") for z in range(PASSES)]

        def load_pass(z):
            nc.sync.dma_start(out=word_table[z][:], in_=x_words[z].rearrange("p n t -> p (n t)").bitcast(I32))
            rows = w1[z * P * PACK : (z + 1) * P * PACK, :]
            nc.sync.dma_start(out=w_raw[z][:], in_=rows.rearrange("(p j) m -> p j m", j=PACK))

        scores = sb.tile([P, D, 2 * PACK], F32, name="scores")[:, :, 0:PACK]
        nc.sync.dma_start(out=scores, in_=score[:, 0, :].rearrange("d (p j) -> p d j", j=PACK))
        picked = load_list("picked", offs)
        neighbours = [load_list("places0", pos1)]
        load_scales()
        load_pass(0)
        load_pass(1)
        neighbours.append(load_list("places1", pos2))
        neighbours.append(load_list("places2", pos3))

        warm_in = sb.tile([P, 1], F32, name="warm_in")
        nc.vector.memset(warm_in[:], 0.0)
        warm_out = sb.tile([P, 1], F32, name="warm_out")
        nc.scalar.activation(warm_out[:], warm_in[:], ACT.Exp)

        ident = sb.tile([P, P], F32, name="ident")
        make_identity(nc, ident[:])

        shape = [P, D, PACK, D]
        gaps = sb.tile(shape, F32, name="gaps")
        nc.vector.tensor_tensor(
            gaps[:],
            scores.rearrange("p r j -> p j r").unsqueeze(1).to_broadcast(shape),
            scores.unsqueeze(3).to_broadcast(shape),
            ALU.subtract,
        )
        ratios = sb.tile(shape, F32, name="ratios", tag="ratios_then_x_scale", align_bytes=64)
        nc.scalar.activation(ratios[:], gaps[:], ACT.Exp)
        total = sb.tile([P, D, PACK], F32, name="total")
        nc.vector.tensor_reduce(total[:], ratios[:], AX.X, ALU.add)
        alpha = sb.tile([P, D, PACK], F32, name="alpha")
        nc.vector.reciprocal(alpha[:], total[:])

        alpha_rows = []
        for d in range(D):
            spread = ps.tile([P, PACK, P], F32, name=f"spread{d}", tag=f"aux{d}")
            for j in range(PACK):
                nc.tensor.transpose(spread[:, j, :], alpha[:, d, j : j + 1].to_broadcast([P, P]), ident[:])
            row = sb.tile([P, V], F32, name=f"alpha_row{d}")
            nc.scalar.copy(row[:].rearrange("p (n j) -> p n j", j=PACK), spread[:].rearrange("p j n -> p n j"))
            alpha_rows.append(row)

        x_scale = sb.tile([P, S], U8, name="x_scale", tag="ratios_then_x_scale", align_bytes=64)
        nc.vector.tensor_copy(x_scale[:], scale_table[:].indirect(picked[:]))
        x_codes0 = sb.tile([P, S], U32, name="x_codes0", align_bytes=64)
        nc.vector.tensor_copy(x_codes0[:], word_table[0][:].bitcast(U32).indirect(picked[:]))

        w_codes = [sb.tile([P, PASSES * P], U32, name=f"w_codes{b}", align_bytes=64) for b in range(BLOCKS)]
        w_scale = [sb.tile([P, PASSES * P], U8, name=f"w_scale{b}", align_bytes=64) for b in range(BLOCKS)]

        def round_weights(grouped, b, z):
            nc.scalar.copy(
                grouped.rearrange("p (c i) j -> p c j i", i=4),
                w_raw[z][:, :, b * P : (b + 1) * P].rearrange("p j (c i) -> p c j i", i=4),
            )

        def product_pass(acc, b, z, codes, lo, hi):
            nc.tensor.matmul_mx(
                out=acc,
                lhsT=w_codes[b][:, z * P : (z + 1) * P].bitcast(FP8X4),
                lhsT_scale=w_scale[b][:, z * P : (z + 1) * P],
                rhs=codes.bitcast(FP8X4),
                rhs_scale=x_scale[4 * z : P, lo:hi],
                start=(z == 0),
                stop=(z == PASSES - 1),
            )

        grouped1 = sb.tile([P, PASSES, P, PACK], BF16, name="grouped1", align_bytes=64)
        for z in range(PASSES):
            grouped0 = sb.tile([P, P, PACK], BF16, name=f"grouped0_{z}", tag=f"staged{z}", align_bytes=64)
            round_weights(grouped0[:], 0, z)
            cols = slice(z * P, (z + 1) * P)
            nc.vector.quantize_mx(
                out=w_codes[0][:, cols].bitcast(FP8X4), scales=w_scale[0][:, cols], in_=grouped0[:].rearrange("p m j -> p (m j)")
            )
            round_weights(grouped1[:, z], 1, z)

        y = [sb.tile([P, S], F32, name=f"y{b}") for b in range(BLOCKS)]
        acc0 = [ps.tile([P, hi - lo], F32, name=f"acc0_{lo}", tag=f"acc0_{lo}") for lo, hi in PIECES]
        for acc, (lo, hi) in zip(acc0, PIECES):
            product_pass(acc[:], 0, 0, x_codes0[:, lo:hi], lo, hi)
        x_codes1 = []
        for tag, (lo, hi) in zip(("staged0", "middle", "staged1"), PIECES):
            piece = sb.tile([P, hi - lo], U32, name=f"x_codes1_{lo}", tag=tag, align_bytes=64)
            nc.vector.tensor_copy(piece[:], word_table[1][:].bitcast(U32).indirect(entries(picked, lo, hi)))
            x_codes1.append(piece)
        nc.vector.quantize_mx(
            out=w_codes[1][:].bitcast(FP8X4), scales=w_scale[1][:], in_=grouped1[:].rearrange("p z m j -> p (z m j)")
        )
        for acc, piece, (lo, hi) in zip(acc0, x_codes1, PIECES):
            product_pass(acc[:], 0, 1, piece[:], lo, hi)
            if lo == 0:
                nc.vector.tensor_copy(y[0][:, lo:hi], acc[:])
            else:
                nc.scalar.copy(y[0][:, lo:hi], acc[:])
        for bank in range(2):
            acc = ps.tile([P, 512], F32, name=f"acc1_{bank}")
            for piece, (lo, hi) in zip(x_codes1, PIECES):
                if lo // 512 == bank:
                    part = acc[:, lo % 512 : lo % 512 + hi - lo]
                    product_pass(part, 1, 0, x_codes0[:, lo:hi], lo, hi)
                    product_pass(part, 1, 1, piece[:], lo, hi)
            nc.scalar.copy(y[1][:, bank * 512 : (bank + 1) * 512], acc[:])

        def weighted(term, b, d, lo, hi):
            nc.vector.tensor_tensor(term, y[b][:].indirect(entries(neighbours[d], lo, hi)), alpha_rows[d][:, lo:hi], ALU.mult)

        def sum_on_tensor(b, lo, hi, tags):
            width = hi - lo
            chunks = width // P
            turned = ps.tile([P, chunks, P], F32, name=f"turned{b}", tag=tags[0])
            for d in range(D):
                term = sb.tile([P, width], F32, name=f"term{b}_{d}")
                weighted(term[:], b, d, lo, hi)
                for c in range(chunks):
                    nc.tensor.matmul(
                        turned[:, c, :], term[:, c * P : (c + 1) * P], ident[:], is_transpose=True,
                        start=(d == 0 and c == 0), stop=(d == D - 1 and c == chunks - 1),
                    )
            rectified = sb.tile([P, width], F32, name=f"rectified{b}")
            nc.scalar.activation(rectified[:], turned[:].rearrange("p c m -> p (c m)"), ACT.Relu)
            back = ps.tile([P, chunks, P], F32, name=f"back{b}", tag=tags[1])
            for c in range(chunks):
                nc.tensor.transpose(back[:, c, :], rectified[:, c * P : (c + 1) * P], ident[:])
            result = sb.tile([P, width], F32, name=f"result{b}")
            nc.scalar.copy(result[:], back[:].rearrange("p c v -> p (c v)"))
            nc.sync.dma_start(out=out[b * P : (b + 1) * P, lo:hi], in_=result[:])

        half = V // 2
        sum_on_tensor(0, 0, V, ("aux0", "aux1"))
        sum_on_tensor(1, 0, half, ("aux2", "acc0_0"))

        terms = [sb.tile([P, half], F32, name=f"last_term{d}") for d in range(D)]
        weighted(terms[0][:], 1, 0, half, V)
        weighted(terms[1][:], 1, 1, half, V)
        weighted(terms[2][:, 0:P], 1, 2, half, half + P)
        partial = sb.tile([P, half], F32, name="partial")
        nc.vector.tensor_tensor(partial[:], terms[0][:], terms[1][:], ALU.add)
        weighted(terms[2][:, P:half], 1, 2, half + P, V)
        summed = sb.tile([P, half], F32, name="summed")
        last = sb.tile([P, half], F32, name="last")
        for lo in (0, P):
            nc.vector.tensor_tensor(summed[:, lo : lo + P], partial[:, lo : lo + P], terms[2][:, lo : lo + P], ALU.add)
        for lo in (0, P):
            nc.vector.tensor_scalar_max(last[:, lo : lo + P], summed[:, lo : lo + P], 0.0)
        nc.sync.dma_start(out=out[P : 2 * P, half:V], in_=last[:])
